import numpy as np
import ml_dtypes


def mxq(x, axis, fmt="e4m3"):
    dtype, down = {"e4m3": (ml_dtypes.float8_e4m3fn, 7), "e5m2": (ml_dtypes.float8_e5m2, 14)}[fmt]
    v = np.moveaxis(np.asarray(x, np.float32).astype(ml_dtypes.bfloat16).astype(np.float64), axis, -1)
    blocks = v.reshape(v.shape[:-1] + (-1, 32))
    amax = np.abs(blocks).max(-1, keepdims=True)
    byte = np.maximum(np.where(amax > 0, np.frexp(amax)[1] - 1 + 127, 0) - down, 1)
    scale = np.exp2(byte - 127.0)
    codes = (blocks / scale).astype(np.float32).astype(dtype).astype(np.float64)
    return np.moveaxis((codes * scale).reshape(v.shape), -1, axis)


WIDE = False


def mx_kscale(k):
    if not WIDE:
        return np.ones(k)
    levels = np.array([10, -10, 5, -5, 0])
    if k % 512:
        return np.exp2(np.random.permutation(np.resize(levels, k // 32))).repeat(32)
    a = np.empty((k // 512, 16))
    for p in range(k // 512):
        a[p, :8] = np.random.permutation(np.resize(levels, 8))
        for g in range(8):
            far = levels[np.abs(levels - a[p, g]) >= 10]
            a[p, g + 8] = far[np.random.randint(len(far))]
    return np.exp2(a.ravel()).repeat(32)


def f64(x):
    return np.asarray(x).astype(np.float64)


def striped(idx):
    return np.tile(idx.reshape(-1, 16).T, (8, 1)).astype(np.uint16)


def unstriped(offs):
    return offs[:16].T.reshape(-1).astype(np.int64)


E2M1 = np.array([0.0, 0.5, 1.0, 1.5, 2.0, 3.0, 4.0, 6.0, -0.0, -0.5, -1.0, -1.5, -2.0, -3.0, -4.0, -6.0])


def pack_weight(w, fmt):
    k, n = w.shape
    w = f64(np.asarray(w, np.float32).astype(ml_dtypes.bfloat16)).reshape(k // 32, 32, n)
    amax = np.abs(w).max(1)
    if fmt == "e4m3":
        byte = np.frexp(amax)[1] - 1 + 127 - 7
    else:
        mant, ex = np.frexp(amax / 6.0)
        byte = np.where(mant > 0.5, ex, ex - 1) + 127
    byte = np.clip(np.where(amax > 0, byte, 1), 1, 254)
    scaled = (w * np.exp2(127.0 - byte)[:, None, :]).reshape(k, n).astype(np.float32)
    by_word = np.ascontiguousarray(scaled.reshape(k // 512, 128, 4, n).transpose(0, 1, 3, 2))
    if fmt == "e4m3":
        words = by_word.astype(ml_dtypes.float8_e4m3fn).view(np.uint8)
    else:
        c = by_word.astype(ml_dtypes.float4_e2m1fn).view(np.uint8) & 0xF
        words = (c[..., 0::2] | (c[..., 1::2] << 4)).reshape(k // 512, 128, 2 * n)
    return np.ascontiguousarray(words), np.ascontiguousarray(byte.astype(np.uint8).reshape(k // 512, 16, n))


def unpack_weight(words, scales, fmt):
    g, _, n = scales.shape
    words = np.ascontiguousarray(words).reshape(g, 128, n, -1)
    if fmt == "e4m3":
        vals = words.view(ml_dtypes.float8_e4m3fn).astype(np.float64)
    else:
        nib = np.empty((g, 128, n, 4), np.uint8)
        nib[..., 0::2] = words & 0xF
        nib[..., 1::2] = words >> 4
        vals = E2M1[nib]
    vals = vals * np.repeat(np.exp2(scales.astype(np.float64) - 127.0), 8, axis=1)[..., None]
    return vals.transpose(0, 1, 3, 2).reshape(g * 512, n)


def silu(v):
    return v / (1.0 + np.exp(-np.maximum(v, -700.0)))


K, T, E, C, H, N = 1536, 1024, 2, 256, 512, 256


def by_expert(wq, xq):
    return np.concatenate([wq[e].T @ xq[:, e * C:(e + 1) * C] for e in range(E)], axis=1)


def setup_inputs():
    n = np.random.standard_normal
    s = mx_kscale(K)[:, None]
    u = mx_kscale(H)
    w1 = [pack_weight(m, "e2m1") for m in n((E, K, H)) / np.sqrt(K) / s[None]]
    w3 = [pack_weight(m, "e2m1") for m in n((E, K, H)) / np.sqrt(K) / s[None] * u[None, None, :]]
    w2 = [pack_weight(m, "e2m1") for m in n((E, H, N)) / np.sqrt(H) / u[None, :, None]]
    x = pack_weight(n((K, T)) * s, "e4m3")
    return {
        "x_words": x[0],
        "x_scales": x[1],
        "w1_words": np.stack([m[0] for m in w1]),
        "w1_scales": np.stack([m[1] for m in w1]),
        "w3_words": np.stack([m[0] for m in w3]),
        "w3_scales": np.stack([m[1] for m in w3]),
        "w2_words": np.stack([m[0] for m in w2]),
        "w2_scales": np.stack([m[1] for m in w2]),
        "gate": np.tile(np.random.uniform(0.2, 1.0, E * C), (N, 1)).astype(np.float32),
        "offs": striped(np.random.permutation(T)[:E * C]),
    }


def reference(x_words, x_scales, w1_words, w1_scales, w3_words, w3_scales, w2_words, w2_scales, gate, offs):
    idx = unstriped(offs)
    w1 = np.stack([unpack_weight(w1_words[e], w1_scales[e], "e2m1") for e in range(E)])
    w3 = np.stack([unpack_weight(w3_words[e], w3_scales[e], "e2m1") for e in range(E)])
    w2 = np.stack([unpack_weight(w2_words[e], w2_scales[e], "e2m1") for e in range(E)])
    xq = unpack_weight(x_words, x_scales, "e4m3")[:, idx]
    h = silu(by_expert(w1, xq))
    h = h * by_expert(w3, xq)
    y = by_expert(w2, mxq(h, 0, "e4m3"))
    out = np.zeros((N, T))
    out[:, idx] = f64(gate) * y
    return out

@@ -1,0 +1,191 @@
+from contextlib import ExitStack
+
+import concourse.mybir as mybir
+from concourse.masks import make_identity
+
+K, T, E, C, H, N = 1536, 1024, 2, 256, 512, 256
+FLOPS = 2 * E * C * (2 * K * H + H * N)
+
+F32 = mybir.dt.float32
+BF16 = mybir.dt.bfloat16
+I32 = mybir.dt.int32
+U32 = mybir.dt.uint32
+U16 = mybir.dt.uint16
+U8 = mybir.dt.uint8
+FP8X4 = mybir.dt.float8_e4m3fn_x4
+FP4X4 = mybir.dt.float4_e2m1fn_x4
+MULT = mybir.AluOpType.mult
+SILU = mybir.ActivationFunctionType.Silu
+
+P = 128
+PASSES = K // 512
+BLOCKS = C // P
+ROW_BLOCKS = N // P
+LIST_ROWS = 16
+
+
+def load_scale_rows(nc, plane, rows):
+    groups = rows.shape[1]
+    by_place = rows.rearrange("(q r) g w -> r q g w", r=4)
+    for r in range(4):
+        nc.sync.dma_start(
+            out=plane[r:P:32, :].bitcast(I32).rearrange("q (g w) -> q g w", g=groups),
+            in_=by_place[r].bitcast(I32),
+        )
+
+
+def tile_moe_pkd_glu_silu_kernel(
+    tc, x_words, x_scales, w1_words, w1_scales, w3_words, w3_scales, w2_words, w2_scales, gate, offs, out
+):
+    nc = tc.nc
+    with ExitStack() as ctx:
+        keep = ctx.enter_context(tc.tile_pool(name="keep", bufs=1))
+        work = ctx.enter_context(tc.tile_pool(name="work", bufs=4))
+        psum = ctx.enter_context(tc.psum_pool(name="psum", bufs=1))
+
+        offsets = keep.tile([P, E * C // LIST_ROWS], U16, name="offsets")
+        x_planes = keep.tile([P, PASSES * T], U8, name="x_planes", align_bytes=64)
+        w1_planes = keep.tile([P, E * PASSES * H], U8, name="w1_planes", align_bytes=64)
+        w3_planes = keep.tile([P, E * PASSES * H], U8, name="w3_planes", align_bytes=64)
+        w2_planes = keep.tile([P, E * N], U8, name="w2_planes", align_bytes=64)
+        x_codes = [keep.tile([P, T], I32, name=f"x_codes{o}", align_bytes=64) for o in range(PASSES)]
+        w1_codes = [keep.tile([P, PASSES * 2 * H], U8, name=f"w1_codes{e}", align_bytes=64) for e in range(E)]
+        w3_codes = [keep.tile([P, PASSES * 2 * H], U8, name=f"w3_codes{e}", align_bytes=64) for e in range(E)]
+        w2_codes = keep.tile([P, E * 2 * N], U8, name="w2_codes", align_bytes=64)
+        gates = keep.tile([P, E * C], F32, name="gates")
+        results = [keep.tile([P, T], F32, name=f"results{b}") for b in range(ROW_BLOCKS)]
+        identity = keep.tile([P, P], F32, name="identity")
+        warm = keep.tile([P, 1], F32, name="warm")
+
+        for plane in (x_planes, w1_planes, w3_planes, w2_planes):
+            nc.vector.memset(plane[:].bitcast(I32), 0)
+        for tile in results:
+            nc.vector.memset(tile[:], 0.0)
+        make_identity(nc, identity[:])
+        nc.scalar.activation(warm[:], identity[:, 0:1], SILU)
+
+        def load_tokens(o):
+            nc.sync.dma_start(out=x_codes[o][:], in_=x_words[o].rearrange("p t r -> p (t r)").bitcast(I32))
+
+        def load_words(tile, words):
+            nc.sync.dma_start(
+                out=tile[:].bitcast(I32).rearrange("p (s w) -> p s w", s=words.shape[0]),
+                in_=words.rearrange("s p w -> p s w").bitcast(I32),
+            )
+
+        nc.sync.dma_start(offsets[:], offs)
+        load_tokens(0)
+        load_scale_rows(nc, x_planes, x_scales.rearrange("o f t -> f o t"))
+        load_words(w1_codes[0], w1_words[0])
+        load_scale_rows(nc, w1_planes, w1_scales.rearrange("e s f i -> f (e s) i"))
+        load_words(w3_codes[0], w3_words[0])
+        load_scale_rows(nc, w3_planes, w3_scales.rearrange("e s f i -> f (e s) i"))
+        load_tokens(1)
+        load_tokens(2)
+        load_words(w1_codes[1], w1_words[1])
+        load_words(w3_codes[1], w3_words[1])
+        load_scale_rows(nc, w2_planes, w2_scales.rearrange("e s f n -> f (e s) n"))
+        load_words(w2_codes, w2_words.rearrange("e s p w -> (e s) p w"))
+        nc.sync.dma_start(out=gates[:], in_=gate[0:P, :])
+
+        slot_codes = {}
+        slot_planes = {}
+        for e in range(E):
+            listed = offsets[:, e * C // LIST_ROWS : (e + 1) * C // LIST_ROWS]
+            for o in range(PASSES):
+                slot_planes[e, o] = keep.tile([P, C], U8, name=f"slot_planes{e}{o}", align_bytes=64)
+                slot_codes[e, o] = keep.tile([P, C], U32, name=f"slot_codes{e}{o}", align_bytes=64)
+                nc.vector.tensor_copy(slot_codes[e, o][:], x_codes[o][:].bitcast(U32).indirect(listed))
+                nc.vector.tensor_copy(slot_planes[e, o][:], x_planes[:, o * T : (o + 1) * T].indirect(listed))
+
+        sums = {}
+
+        def first_layer(e, blocks):
+            for b in blocks:
+                pair = (e * BLOCKS + b) % 3
+                sums[e, b] = [psum.tile([P, H], F32, name=f"sums{pair}{m}") for m in range(2)]
+            for o in range(PASSES):
+                for b in blocks:
+                    slots = slice(b * P, (b + 1) * P)
+                    for m, (codes, planes) in enumerate(((w1_codes, w1_planes), (w3_codes, w3_planes))):
+                        at = (e * PASSES + o) * H
+                        nc.tensor.matmul_mx(
+                            out=sums[e, b][m][:],
+                            lhsT=slot_codes[e, o][:, slots].bitcast(FP8X4),
+                            lhsT_scale=slot_planes[e, o][:, slots],
+                            rhs=codes[e][:, o * 2 * H : (o + 1) * 2 * H].bitcast(FP4X4),
+                            rhs_scale=planes[:, at : at + H],
+                            start=(o == 0),
+                            stop=(o == PASSES - 1),
+                        )
+
+        hidden = {}
+
+        def activate(e, b):
+            a, g = (s[:].rearrange("s (p u v) -> s u p v", u=2, v=2) for s in sums[e, b])
+            act = work.tile([P, H], F32, name="act")
+            nc.scalar.activation(act[:].rearrange("s (u p v) -> s u p v", u=2, v=2), a, SILU)
+            hidden[e, b] = work.tile([P, H], BF16, name="hidden")
+            nc.vector.tensor_tensor(
+                hidden[e, b][:].rearrange("s (u p v) -> s u p v", u=2, v=2),
+                g,
+                act[:].rearrange("s (u p v) -> s u p v", u=2, v=2),
+                MULT,
+            )
+
+        h_codes = {}
+        h_planes = {}
+
+        def turn_and_quantise(e, b):
+            pairs = hidden[e, b][:].bitcast(F32)
+            turned = psum.tile([P, 2, P], F32, name="turned")
+            for u in range(2):
+                nc.tensor.transpose(turned[:, u, :], pairs[:, u * P : (u + 1) * P], identity[:])
+            grouped = work.tile([P, 4 * P], BF16, name="grouped", align_bytes=64)
+            nc.scalar.copy(
+                grouped[:].bitcast(F32).rearrange("p (s u) -> p s u", u=2),
+                turned[:].rearrange("p u s -> p s u"),
+            )
+            h_codes[e, b] = work.tile([P, P], U32, name="h_codes", align_bytes=64)
+            h_planes[e, b] = work.tile([P, P], U8, name="h_planes", align_bytes=64)
+            nc.vector.quantize_mx(out=h_codes[e, b][:].bitcast(FP8X4), scales=h_planes[e, b][:], in_=grouped[:])
+
+        def second_layer(e, b):
+            y = psum.tile([P, ROW_BLOCKS, P], F32, name="y")
+            for r in range(ROW_BLOCKS):
+                at = e * N + r * P
+                nc.tensor.matmul_mx(
+                    out=y[:, r, :],
+                    lhsT=w2_codes[:, 2 * at : 2 * (at + P)].bitcast(FP4X4),
+                    lhsT_scale=w2_planes[:, at : at + P],
+                    rhs=h_codes[e, b][:].bitcast(FP8X4),
+                    rhs_scale=h_planes[e, b][:],
+                    start=True,
+                    stop=True,
+                )
+            staged = work.tile([P, ROW_BLOCKS, P], F32, name="staged")
+            nc.scalar.copy(staged[:], y[:])
+            first = e * C + b * P
+            listed = offsets[:, first // LIST_ROWS : (first + P) // LIST_ROWS]
+            for r in range(ROW_BLOCKS):
+                nc.vector.tensor_tensor(
+                    results[r][:].indirect(listed), staged[:, r, :], gates[:, first : first + P], MULT
+                )
+
+        first_layer(0, (0, 1))
+        activate(0, 0)
+        activate(0, 1)
+        first_layer(1, (0,))
+        turn_and_quantise(0, 0)
+        turn_and_quantise(0, 1)
+        first_layer(1, (1,))
+        second_layer(0, 0)
+        activate(1, 0)
+        second_layer(0, 1)
+        activate(1, 1)
+        turn_and_quantise(1, 0)
+        turn_and_quantise(1, 1)
+        second_layer(1, 0)
+        second_layer(1, 1)
+        for r in range(ROW_BLOCKS):
+            nc.sync.dma_start(out=out[r * P : (r + 1) * P, :], in_=results[r][:])

@@ -21,17 +21,26 @@ P = 128
 PASSES = K // 512
 BLOCKS = C // P
 ROW_BLOCKS = N // P
-LIST_ROWS = 16
+SLOTS_A_COLUMN = 16
+SCALE_ROWS = 4
+SUM_PAIRS = 3
+ALIGN = 64
 
 
-def load_scale_rows(nc, plane, rows):
-    groups = rows.shape[1]
-    by_place = rows.rearrange("(q r) g w -> r q g w", r=4)
-    for r in range(4):
+def load_scale_rows(nc, planes, rows):
+    by_place = rows.rearrange("(q r) g w -> r q g w", r=SCALE_ROWS)
+    for r in range(SCALE_ROWS):
         nc.sync.dma_start(
-            out=plane[r:P:32, :].bitcast(I32).rearrange("q (g w) -> q g w", g=groups),
+            out=planes[r:P:32, :].bitcast(I32).rearrange("q (g w) -> q g w", g=rows.shape[1]),
             in_=by_place[r].bitcast(I32),
         )
+
+
+def load_words(nc, tile, words):
+    nc.sync.dma_start(
+        out=tile[:].bitcast(I32).rearrange("p (s w) -> p s w", s=words.shape[0]),
+        in_=words.rearrange("s p w -> p s w").bitcast(I32),
+    )
 
 
 def tile_moe_pkd_glu_silu_kernel(
@@ -40,152 +49,167 @@ def tile_moe_pkd_glu_silu_kernel(
     nc = tc.nc
     with ExitStack() as ctx:
         keep = ctx.enter_context(tc.tile_pool(name="keep", bufs=1))
-        work = ctx.enter_context(tc.tile_pool(name="work", bufs=4))
+        work = ctx.enter_context(tc.tile_pool(name="work", bufs=E * BLOCKS))
         psum = ctx.enter_context(tc.psum_pool(name="psum", bufs=1))
 
-        offsets = keep.tile([P, E * C // LIST_ROWS], U16, name="offsets")
-        x_planes = keep.tile([P, PASSES * T], U8, name="x_planes", align_bytes=64)
-        w1_planes = keep.tile([P, E * PASSES * H], U8, name="w1_planes", align_bytes=64)
-        w3_planes = keep.tile([P, E * PASSES * H], U8, name="w3_planes", align_bytes=64)
-        w2_planes = keep.tile([P, E * N], U8, name="w2_planes", align_bytes=64)
-        x_codes = [keep.tile([P, T], I32, name=f"x_codes{o}", align_bytes=64) for o in range(PASSES)]
-        w1_codes = [keep.tile([P, PASSES * 2 * H], U8, name=f"w1_codes{e}", align_bytes=64) for e in range(E)]
-        w3_codes = [keep.tile([P, PASSES * 2 * H], U8, name=f"w3_codes{e}", align_bytes=64) for e in range(E)]
-        w2_codes = keep.tile([P, E * 2 * N], U8, name="w2_codes", align_bytes=64)
+        offsets = keep.tile([P, E * C // SLOTS_A_COLUMN], U16, name="offsets")
+        x_planes = keep.tile([P, PASSES * T], U8, name="x_planes", align_bytes=ALIGN)
+        w1_planes_both = keep.tile([P, E * PASSES * H], U8, name="w1_planes_both", align_bytes=ALIGN)
+        w1_planes = [w1_planes_both[:, e * PASSES * H : (e + 1) * PASSES * H] for e in range(E)]
+        w3_planes = [keep.tile([P, PASSES * H], U8, name=f"w3_planes{e}", align_bytes=ALIGN) for e in range(E)]
+        w2_planes = keep.tile([P, E * N], U8, name="w2_planes", align_bytes=ALIGN)
+        x_codes = [keep.tile([P, T], I32, name=f"x_codes{o}", tag=f"x_codes{o}", align_bytes=ALIGN) for o in range(PASSES)]
+        w1_codes = [keep.tile([P, PASSES * 2 * H], U8, name=f"w1_codes{e}", align_bytes=ALIGN) for e in range(E)]
+        w3_codes = [keep.tile([P, PASSES * 2 * H], U8, name=f"w3_codes{e}", align_bytes=ALIGN) for e in range(E)]
+        w2_codes = keep.tile([P, E * 2 * N], U8, name="w2_codes", align_bytes=ALIGN)
         gates = keep.tile([P, E * C], F32, name="gates")
-        results = [keep.tile([P, T], F32, name=f"results{b}") for b in range(ROW_BLOCKS)]
+        results = [keep.tile([P, T], F32, name=f"results{r}") for r in range(ROW_BLOCKS)]
         identity = keep.tile([P, P], F32, name="identity")
-        warm = keep.tile([P, 1], F32, name="warm")
+        zero = keep.tile([P, 1], F32, name="zero")
 
-        for plane in (x_planes, w1_planes, w3_planes, w2_planes):
-            nc.vector.memset(plane[:].bitcast(I32), 0)
+        nc.gpsimd.memset(x_planes[:].bitcast(I32), 0)
+        nc.vector.memset(zero[:], 0.0)
+        for planes in (w1_planes_both, w3_planes[0], w2_planes, w3_planes[1]):
+            nc.vector.memset(planes[:].bitcast(I32), 0)
         for tile in results:
-            nc.vector.memset(tile[:], 0.0)
+            nc.scalar.activation(tile[:], zero[:].to_broadcast([P, T]), SILU)
         make_identity(nc, identity[:])
-        nc.scalar.activation(warm[:], identity[:, 0:1], SILU)
 
         def load_tokens(o):
             nc.sync.dma_start(out=x_codes[o][:], in_=x_words[o].rearrange("p t r -> p (t r)").bitcast(I32))
 
-        def load_words(tile, words):
-            nc.sync.dma_start(
-                out=tile[:].bitcast(I32).rearrange("p (s w) -> p s w", s=words.shape[0]),
-                in_=words.rearrange("s p w -> p s w").bitcast(I32),
-            )
-
         nc.sync.dma_start(offsets[:], offs)
         load_tokens(0)
         load_scale_rows(nc, x_planes, x_scales.rearrange("o f t -> f o t"))
-        load_words(w1_codes[0], w1_words[0])
-        load_scale_rows(nc, w1_planes, w1_scales.rearrange("e s f i -> f (e s) i"))
-        load_words(w3_codes[0], w3_words[0])
-        load_scale_rows(nc, w3_planes, w3_scales.rearrange("e s f i -> f (e s) i"))
+        load_scale_rows(nc, w1_planes_both, w1_scales.rearrange("e s f i -> f (e s) i"))
+        load_words(nc, w1_codes[0], w1_words[0])
         load_tokens(1)
         load_tokens(2)
-        load_words(w1_codes[1], w1_words[1])
-        load_words(w3_codes[1], w3_words[1])
+        load_words(nc, w3_codes[0], w3_words[0])
+        load_scale_rows(nc, w3_planes[0], w3_scales[0].rearrange("s f i -> f s i"))
+        load_words(nc, w1_codes[1], w1_words[1])
+        load_words(nc, w2_codes, w2_words.rearrange("e s p w -> (e s) p w"))
         load_scale_rows(nc, w2_planes, w2_scales.rearrange("e s f n -> f (e s) n"))
-        load_words(w2_codes, w2_words.rearrange("e s p w -> (e s) p w"))
+        load_words(nc, w3_codes[1], w3_words[1])
         nc.sync.dma_start(out=gates[:], in_=gate[0:P, :])
+        load_scale_rows(nc, w3_planes[1], w3_scales[1].rearrange("s f i -> f s i"))
+
+        def listed(first, count):
+            return offsets[:, first // SLOTS_A_COLUMN : (first + count) // SLOTS_A_COLUMN]
 
         slot_codes = {}
         slot_planes = {}
-        for e in range(E):
-            listed = offsets[:, e * C // LIST_ROWS : (e + 1) * C // LIST_ROWS]
-            for o in range(PASSES):
-                slot_planes[e, o] = keep.tile([P, C], U8, name=f"slot_planes{e}{o}", align_bytes=64)
-                slot_codes[e, o] = keep.tile([P, C], U32, name=f"slot_codes{e}{o}", align_bytes=64)
-                nc.vector.tensor_copy(slot_codes[e, o][:], x_codes[o][:].bitcast(U32).indirect(listed))
-                nc.vector.tensor_copy(slot_planes[e, o][:], x_planes[:, o * T : (o + 1) * T].indirect(listed))
+        for o in range(PASSES):
+            gathered = keep.tile([P, E * C], U8, name=f"slot_planes{o}", align_bytes=ALIGN)
+            nc.vector.tensor_copy(gathered[:], x_planes[:, o * T : (o + 1) * T].indirect(offsets[:]))
+            for e in range(E):
+                slot_planes[e, o] = gathered[:, e * C : (e + 1) * C]
+
+        def gather_codes(e, o, target):
+            slot_codes[e, o] = target
+            nc.vector.tensor_copy(target, x_codes[o][:].bitcast(U32).indirect(listed(e * C, C)))
+
+        last_pass = PASSES - 1
+        for e, o in [(0, o) for o in range(PASSES)] + [(1, last_pass)]:
+            gather_codes(e, o, keep.tile([P, C], U32, name=f"slot_codes{e}{o}", align_bytes=ALIGN)[:])
+        later_codes = keep.tile([P, last_pass * C], U32, name="later_codes", tag=f"x_codes{last_pass}", align_bytes=ALIGN)
+        for o in range(last_pass):
+            gather_codes(1, o, later_codes[:, o * C : (o + 1) * C])
 
         sums = {}
 
         def first_layer(e, blocks):
             for b in blocks:
-                pair = (e * BLOCKS + b) % 3
-                sums[e, b] = [psum.tile([P, H], F32, name=f"sums{pair}{m}") for m in range(2)]
-            for o in range(PASSES):
+                pair = (e * BLOCKS + b) % SUM_PAIRS
+                sums[e, b] = [psum.tile([P, H], F32, name=f"sums{e}{b}{m}", tag=f"sums{pair}{m}") for m in range(2)]
+            for m, (codes, planes) in enumerate(((w1_codes, w1_planes), (w3_codes, w3_planes))):
                 for b in blocks:
                     slots = slice(b * P, (b + 1) * P)
-                    for m, (codes, planes) in enumerate(((w1_codes, w1_planes), (w3_codes, w3_planes))):
-                        at = (e * PASSES + o) * H
+                    for o in range(PASSES):
                         nc.tensor.matmul_mx(
                             out=sums[e, b][m][:],
                             lhsT=slot_codes[e, o][:, slots].bitcast(FP8X4),
                             lhsT_scale=slot_planes[e, o][:, slots],
                             rhs=codes[e][:, o * 2 * H : (o + 1) * 2 * H].bitcast(FP4X4),
-                            rhs_scale=planes[:, at : at + H],
+                            rhs_scale=planes[e][:, o * H : (o + 1) * H],
                             start=(o == 0),
                             stop=(o == PASSES - 1),
                         )
 
-        hidden = {}
-
-        def activate(e, b):
+        def hidden_values(e, b):
             a, g = (s[:].rearrange("s (p u v) -> s u p v", u=2, v=2) for s in sums[e, b])
-            act = work.tile([P, H], F32, name="act")
-            nc.scalar.activation(act[:].rearrange("s (u p v) -> s u p v", u=2, v=2), a, SILU)
-            hidden[e, b] = work.tile([P, H], BF16, name="hidden")
-            nc.vector.tensor_tensor(
-                hidden[e, b][:].rearrange("s (u p v) -> s u p v", u=2, v=2),
-                g,
-                act[:].rearrange("s (u p v) -> s u p v", u=2, v=2),
-                MULT,
-            )
+            silu_a = keep.tile([P, H], F32, name=f"silu_a{e}{b}", tag=f"silu_a{e}{b}", align_bytes=ALIGN)
+            silu_a_ordered = silu_a[:].rearrange("s (u p v) -> s u p v", u=2, v=2)
+            nc.scalar.activation(silu_a_ordered, a, SILU)
+            hidden = work.tile([P, H], BF16, name="hidden")
+            nc.vector.tensor_tensor(hidden[:].rearrange("s (u p v) -> s u p v", u=2, v=2), g, silu_a_ordered, MULT)
+            return hidden
 
-        h_codes = {}
-        h_planes = {}
-
-        def turn_and_quantise(e, b):
-            pairs = hidden[e, b][:].bitcast(F32)
+        def turn_and_quantise(e, b, hidden):
+            pairs = hidden[:].bitcast(F32)
             turned = psum.tile([P, 2, P], F32, name="turned")
             for u in range(2):
                 nc.tensor.transpose(turned[:, u, :], pairs[:, u * P : (u + 1) * P], identity[:])
-            grouped = work.tile([P, 4 * P], BF16, name="grouped", align_bytes=64)
+            grouped = keep.tile([P, 4 * P], BF16, name=f"grouped{e}{b}", tag=f"grouped{e}{b}", align_bytes=ALIGN)
             nc.scalar.copy(
                 grouped[:].bitcast(F32).rearrange("p (s u) -> p s u", u=2),
                 turned[:].rearrange("p u s -> p s u"),
             )
-            h_codes[e, b] = work.tile([P, P], U32, name="h_codes", align_bytes=64)
-            h_planes[e, b] = work.tile([P, P], U8, name="h_planes", align_bytes=64)
-            nc.vector.quantize_mx(out=h_codes[e, b][:].bitcast(FP8X4), scales=h_planes[e, b][:], in_=grouped[:])
+            h_codes = work.tile([P, P], U32, name="h_codes", align_bytes=ALIGN)
+            h_plane = work.tile([P, P], U8, name="h_plane", align_bytes=ALIGN)
+            nc.vector.quantize_mx(out=h_codes[:].bitcast(FP8X4), scales=h_plane[:], in_=grouped[:])
+            return h_codes, h_plane
 
-        def second_layer(e, b):
-            y = psum.tile([P, ROW_BLOCKS, P], F32, name="y")
+        y_tags = ("y", "sums21", "sums11", "sums10")
+        ys = {}
+
+        def second_layer(e, b, h_codes, h_plane):
+            ys[e, b] = psum.tile([P, ROW_BLOCKS, P], F32, name=f"y{e}{b}", tag=y_tags[e * BLOCKS + b])
             for r in range(ROW_BLOCKS):
-                at = e * N + r * P
+                column = e * N + r * P
                 nc.tensor.matmul_mx(
-                    out=y[:, r, :],
-                    lhsT=w2_codes[:, 2 * at : 2 * (at + P)].bitcast(FP4X4),
-                    lhsT_scale=w2_planes[:, at : at + P],
-                    rhs=h_codes[e, b][:].bitcast(FP8X4),
-                    rhs_scale=h_planes[e, b][:],
+                    out=ys[e, b][:, r, :],
+                    lhsT=w2_codes[:, 2 * column : 2 * (column + P)].bitcast(FP4X4),
+                    lhsT_scale=w2_planes[:, column : column + P],
+                    rhs=h_codes[:].bitcast(FP8X4),
+                    rhs_scale=h_plane[:],
                     start=True,
                     stop=True,
                 )
-            staged = work.tile([P, ROW_BLOCKS, P], F32, name="staged")
-            nc.scalar.copy(staged[:], y[:])
-            first = e * C + b * P
-            listed = offsets[:, first // LIST_ROWS : (first + P) // LIST_ROWS]
-            for r in range(ROW_BLOCKS):
-                nc.vector.tensor_tensor(
-                    results[r][:].indirect(listed), staged[:, r, :], gates[:, first : first + P], MULT
-                )
 
-        first_layer(0, (0, 1))
-        activate(0, 0)
-        activate(0, 1)
-        first_layer(1, (0,))
-        turn_and_quantise(0, 0)
-        turn_and_quantise(0, 1)
-        first_layer(1, (1,))
-        second_layer(0, 0)
-        activate(1, 0)
-        second_layer(0, 1)
-        activate(1, 1)
-        turn_and_quantise(1, 0)
-        turn_and_quantise(1, 1)
-        second_layer(1, 0)
-        second_layer(1, 1)
+        staged = {}
+
+        def stage_block(e, b):
+            rows = keep.tile([P, ROW_BLOCKS, P], F32, name=f"staged{e}{b}")
+            nc.scalar.copy(rows[:], ys[e, b][:])
+            for r in range(ROW_BLOCKS):
+                staged[e, b, r] = rows[:, r, :]
+
+        def stage_rows(e, b, r, tag):
+            rows = keep.tile([P, P], F32, name=f"staged{e}{b}{r}", tag=tag, align_bytes=ALIGN)
+            nc.scalar.copy(rows[:], ys[e, b][:, r, :])
+            staged[e, b, r] = rows[:]
+
+        def expert_1_block(b):
+            first_layer(1, (b,))
+            second_layer(1, b, *turn_and_quantise(1, b, hidden_values(1, b)))
+            stage_block(1, b)
+
+        first_layer(0, range(BLOCKS))
+        quantised = [turn_and_quantise(0, b, hidden_values(0, b)) for b in range(BLOCKS)]
+        second_layer(0, 0, *quantised[0])
+        expert_1_block(0)
+        second_layer(0, 1, *quantised[1])
+        expert_1_block(1)
+        scatters = [(b, r) for b in range(BLOCKS) for r in range(ROW_BLOCKS)]
+        for (b, r), tag in zip(scatters, ("staged_first", "silu_a10", "silu_a11", "grouped10")):
+            stage_rows(0, b, r, tag)
+
         for r in range(ROW_BLOCKS):
+            for e in range(E):
+                for b in range(BLOCKS):
+                    first = e * C + b * P
+                    nc.vector.tensor_tensor(
+                        results[r][:].indirect(listed(first, P)), staged[e, b, r], gates[:, first : first + P], MULT
+                    )
             nc.sync.dma_start(out=out[r * P : (r + 1) * P, :], in_=results[r][:])

@@ -91,8 +91,8 @@ def tile_moe_pkd_glu_silu_kernel(
         load_words(nc, w2_codes, w2_words.rearrange("e s p w -> (e s) p w"))
         load_scale_rows(nc, w2_planes, w2_scales.rearrange("e s f n -> f (e s) n"))
         load_words(nc, w3_codes[1], w3_words[1])
-        nc.sync.dma_start(out=gates[:], in_=gate[0:P, :])
         load_scale_rows(nc, w3_planes[1], w3_scales[1].rearrange("s f i -> f s i"))
+        nc.sync.dma_start(out=gates[:], in_=gate[0:P, :])
 
         def listed(first, count):
             return offsets[:, first // SLOTS_A_COLUMN : (first + count) // SLOTS_A_COLUMN]
@@ -151,7 +151,8 @@ def tile_moe_pkd_glu_silu_kernel(
             for u in range(2):
                 nc.tensor.transpose(turned[:, u, :], pairs[:, u * P : (u + 1) * P], identity[:])
             grouped = keep.tile([P, 4 * P], BF16, name=f"grouped{e}{b}", tag=f"grouped{e}{b}", align_bytes=ALIGN)
-            nc.scalar.copy(
+            copy_words = nc.vector.tensor_copy if e == 0 else nc.scalar.copy
+            copy_words(
                 grouped[:].bitcast(F32).rearrange("p (s u) -> p s u", u=2),
                 turned[:].rearrange("p u s -> p s u"),
             )
@@ -190,17 +191,19 @@ def tile_moe_pkd_glu_silu_kernel(
             nc.scalar.copy(rows[:], ys[e, b][:, r, :])
             staged[e, b, r] = rows[:]
 
-        def expert_1_block(b):
-            first_layer(1, (b,))
-            second_layer(1, b, *turn_and_quantise(1, b, hidden_values(1, b)))
-            stage_block(1, b)
+        def after_first_layer(e, b):
+            second_layer(e, b, *turn_and_quantise(e, b, hidden_values(e, b)))
+            stage_block(e, b)
 
         first_layer(0, range(BLOCKS))
-        quantised = [turn_and_quantise(0, b, hidden_values(0, b)) for b in range(BLOCKS)]
-        second_layer(0, 0, *quantised[0])
-        expert_1_block(0)
-        second_layer(0, 1, *quantised[1])
-        expert_1_block(1)
+        hidden_0 = [hidden_values(0, b) for b in range(BLOCKS)]
+        first_layer(1, (0,))
+        second_layer(0, 0, *turn_and_quantise(0, 0, hidden_0[0]))
+        quantised_01 = turn_and_quantise(0, 1, hidden_0[1])
+        after_first_layer(1, 0)
+        second_layer(0, 1, *quantised_01)
+        first_layer(1, (1,))
+        after_first_layer(1, 1)
         scatters = [(b, r) for b in range(BLOCKS) for r in range(ROW_BLOCKS)]
         for (b, r), tag in zip(scatters, ("staged_first", "silu_a10", "silu_a11", "grouped10")):
             stage_rows(0, b, r, tag)

from contextlib import ExitStack

import concourse.mybir as mybir
from concourse.masks import make_identity

K, T, E, C, H, N = 1536, 1024, 2, 256, 512, 256
FLOPS = 2 * E * C * (2 * K * H + H * N)

F32 = mybir.dt.float32
BF16 = mybir.dt.bfloat16
I32 = mybir.dt.int32
U32 = mybir.dt.uint32
U16 = mybir.dt.uint16
U8 = mybir.dt.uint8
FP8X4 = mybir.dt.float8_e4m3fn_x4
FP4X4 = mybir.dt.float4_e2m1fn_x4
MULT = mybir.AluOpType.mult
SILU = mybir.ActivationFunctionType.Silu

P = 128
PASSES = K // 512
BLOCKS = C // P
ROW_BLOCKS = N // P
SLOTS_A_COLUMN = 16
SCALE_ROWS = 4
SUM_PAIRS = 3
ALIGN = 64


def load_scale_rows(nc, planes, rows):
    by_place = rows.rearrange("(q r) g w -> r q g w", r=SCALE_ROWS)
    for r in range(SCALE_ROWS):
        nc.sync.dma_start(
            out=planes[r:P:32, :].bitcast(I32).rearrange("q (g w) -> q g w", g=rows.shape[1]),
            in_=by_place[r].bitcast(I32),
        )


def load_words(nc, tile, words):
    nc.sync.dma_start(
        out=tile[:].bitcast(I32).rearrange("p (s w) -> p s w", s=words.shape[0]),
        in_=words.rearrange("s p w -> p s w").bitcast(I32),
    )


def tile_moe_pkd_glu_silu_kernel(
    tc, x_words, x_scales, w1_words, w1_scales, w3_words, w3_scales, w2_words, w2_scales, gate, offs, out
):
    nc = tc.nc
    with ExitStack() as ctx:
        keep = ctx.enter_context(tc.tile_pool(name="keep", bufs=1))
        work = ctx.enter_context(tc.tile_pool(name="work", bufs=E * BLOCKS))
        psum = ctx.enter_context(tc.psum_pool(name="psum", bufs=1))

        offsets = keep.tile([P, E * C // SLOTS_A_COLUMN], U16, name="offsets")
        x_planes = keep.tile([P, PASSES * T], U8, name="x_planes", align_bytes=ALIGN)
        w1_planes_both = keep.tile([P, E * PASSES * H], U8, name="w1_planes_both", align_bytes=ALIGN)
        w1_planes = [w1_planes_both[:, e * PASSES * H : (e + 1) * PASSES * H] for e in range(E)]
        w3_planes = [keep.tile([P, PASSES * H], U8, name=f"w3_planes{e}", align_bytes=ALIGN) for e in range(E)]
        w2_planes = keep.tile([P, E * N], U8, name="w2_planes", align_bytes=ALIGN)
        x_codes = [keep.tile([P, T], I32, name=f"x_codes{o}", tag=f"x_codes{o}", align_bytes=ALIGN) for o in range(PASSES)]
        w1_codes = [keep.tile([P, PASSES * 2 * H], U8, name=f"w1_codes{e}", align_bytes=ALIGN) for e in range(E)]
        w3_codes = [keep.tile([P, PASSES * 2 * H], U8, name=f"w3_codes{e}", align_bytes=ALIGN) for e in range(E)]
        w2_codes = keep.tile([P, E * 2 * N], U8, name="w2_codes", align_bytes=ALIGN)
        gates = keep.tile([P, E * C], F32, name="gates")
        results = [keep.tile([P, T], F32, name=f"results{r}") for r in range(ROW_BLOCKS)]
        identity = keep.tile([P, P], F32, name="identity")
        zero = keep.tile([P, 1], F32, name="zero")

        nc.gpsimd.memset(x_planes[:].bitcast(I32), 0)
        nc.vector.memset(zero[:], 0.0)
        for planes in (w1_planes_both, w3_planes[0], w2_planes, w3_planes[1]):
            nc.vector.memset(planes[:].bitcast(I32), 0)
        for tile in results:
            nc.scalar.activation(tile[:], zero[:].to_broadcast([P, T]), SILU)
        make_identity(nc, identity[:])

        def load_tokens(o):
            nc.sync.dma_start(out=x_codes[o][:], in_=x_words[o].rearrange("p t r -> p (t r)").bitcast(I32))

        nc.sync.dma_start(offsets[:], offs)
        load_tokens(0)
        load_scale_rows(nc, x_planes, x_scales.rearrange("o f t -> f o t"))
        load_scale_rows(nc, w1_planes_both, w1_scales.rearrange("e s f i -> f (e s) i"))
        load_words(nc, w1_codes[0], w1_words[0])
        load_tokens(1)
        load_tokens(2)
        load_words(nc, w3_codes[0], w3_words[0])
        load_scale_rows(nc, w3_planes[0], w3_scales[0].rearrange("s f i -> f s i"))
        load_words(nc, w1_codes[1], w1_words[1])
        load_words(nc, w2_codes, w2_words.rearrange("e s p w -> (e s) p w"))
        load_scale_rows(nc, w2_planes, w2_scales.rearrange("e s f n -> f (e s) n"))
        load_words(nc, w3_codes[1], w3_words[1])
        load_scale_rows(nc, w3_planes[1], w3_scales[1].rearrange("s f i -> f s i"))
        nc.sync.dma_start(out=gates[:], in_=gate[0:P, :])

        def listed(first, count):
            return offsets[:, first // SLOTS_A_COLUMN : (first + count) // SLOTS_A_COLUMN]

        slot_codes = {}
        slot_planes = {}
        for o in range(PASSES):
            gathered = keep.tile([P, E * C], U8, name=f"slot_planes{o}", align_bytes=ALIGN)
            nc.vector.tensor_copy(gathered[:], x_planes[:, o * T : (o + 1) * T].indirect(offsets[:]))
            for e in range(E):
                slot_planes[e, o] = gathered[:, e * C : (e + 1) * C]

        def gather_codes(e, o, target):
            slot_codes[e, o] = target
            nc.vector.tensor_copy(target, x_codes[o][:].bitcast(U32).indirect(listed(e * C, C)))

        last_pass = PASSES - 1
        for e, o in [(0, o) for o in range(PASSES)] + [(1, last_pass)]:
            gather_codes(e, o, keep.tile([P, C], U32, name=f"slot_codes{e}{o}", align_bytes=ALIGN)[:])
        later_codes = keep.tile([P, last_pass * C], U32, name="later_codes", tag=f"x_codes{last_pass}", align_bytes=ALIGN)
        for o in range(last_pass):
            gather_codes(1, o, later_codes[:, o * C : (o + 1) * C])

        sums = {}

        def first_layer(e, blocks):
            for b in blocks:
                pair = (e * BLOCKS + b) % SUM_PAIRS
                sums[e, b] = [psum.tile([P, H], F32, name=f"sums{e}{b}{m}", tag=f"sums{pair}{m}") for m in range(2)]
            for m, (codes, planes) in enumerate(((w1_codes, w1_planes), (w3_codes, w3_planes))):
                for b in blocks:
                    slots = slice(b * P, (b + 1) * P)
                    for o in range(PASSES):
                        nc.tensor.matmul_mx(
                            out=sums[e, b][m][:],
                            lhsT=slot_codes[e, o][:, slots].bitcast(FP8X4),
                            lhsT_scale=slot_planes[e, o][:, slots],
                            rhs=codes[e][:, o * 2 * H : (o + 1) * 2 * H].bitcast(FP4X4),
                            rhs_scale=planes[e][:, o * H : (o + 1) * H],
                            start=(o == 0),
                            stop=(o == PASSES - 1),
                        )

        def hidden_values(e, b):
            a, g = (s[:].rearrange("s (p u v) -> s u p v", u=2, v=2) for s in sums[e, b])
            silu_a = keep.tile([P, H], F32, name=f"silu_a{e}{b}", tag=f"silu_a{e}{b}", align_bytes=ALIGN)
            silu_a_ordered = silu_a[:].rearrange("s (u p v) -> s u p v", u=2, v=2)
            nc.scalar.activation(silu_a_ordered, a, SILU)
            hidden = work.tile([P, H], BF16, name="hidden")
            nc.vector.tensor_tensor(hidden[:].rearrange("s (u p v) -> s u p v", u=2, v=2), g, silu_a_ordered, MULT)
            return hidden

        def turn_and_quantise(e, b, hidden):
            pairs = hidden[:].bitcast(F32)
            turned = psum.tile([P, 2, P], F32, name="turned")
            for u in range(2):
                nc.tensor.transpose(turned[:, u, :], pairs[:, u * P : (u + 1) * P], identity[:])
            grouped = keep.tile([P, 4 * P], BF16, name=f"grouped{e}{b}", tag=f"grouped{e}{b}", align_bytes=ALIGN)
            copy_words = nc.vector.tensor_copy if e == 0 else nc.scalar.copy
            copy_words(
                grouped[:].bitcast(F32).rearrange("p (s u) -> p s u", u=2),
                turned[:].rearrange("p u s -> p s u"),
            )
            h_codes = work.tile([P, P], U32, name="h_codes", align_bytes=ALIGN)
            h_plane = work.tile([P, P], U8, name="h_plane", align_bytes=ALIGN)
            nc.vector.quantize_mx(out=h_codes[:].bitcast(FP8X4), scales=h_plane[:], in_=grouped[:])
            return h_codes, h_plane

        y_tags = ("y", "sums21", "sums11", "sums10")
        ys = {}

        def second_layer(e, b, h_codes, h_plane):
            ys[e, b] = psum.tile([P, ROW_BLOCKS, P], F32, name=f"y{e}{b}", tag=y_tags[e * BLOCKS + b])
            for r in range(ROW_BLOCKS):
                column = e * N + r * P
                nc.tensor.matmul_mx(
                    out=ys[e, b][:, r, :],
                    lhsT=w2_codes[:, 2 * column : 2 * (column + P)].bitcast(FP4X4),
                    lhsT_scale=w2_planes[:, column : column + P],
                    rhs=h_codes[:].bitcast(FP8X4),
                    rhs_scale=h_plane[:],
                    start=True,
                    stop=True,
                )

        staged = {}

        def stage_block(e, b):
            rows = keep.tile([P, ROW_BLOCKS, P], F32, name=f"staged{e}{b}")
            nc.scalar.copy(rows[:], ys[e, b][:])
            for r in range(ROW_BLOCKS):
                staged[e, b, r] = rows[:, r, :]

        def stage_rows(e, b, r, tag):
            rows = keep.tile([P, P], F32, name=f"staged{e}{b}{r}", tag=tag, align_bytes=ALIGN)
            nc.scalar.copy(rows[:], ys[e, b][:, r, :])
            staged[e, b, r] = rows[:]

        def after_first_layer(e, b):
            second_layer(e, b, *turn_and_quantise(e, b, hidden_values(e, b)))
            stage_block(e, b)

        first_layer(0, range(BLOCKS))
        hidden_0 = [hidden_values(0, b) for b in range(BLOCKS)]
        first_layer(1, (0,))
        second_layer(0, 0, *turn_and_quantise(0, 0, hidden_0[0]))
        quantised_01 = turn_and_quantise(0, 1, hidden_0[1])
        after_first_layer(1, 0)
        second_layer(0, 1, *quantised_01)
        first_layer(1, (1,))
        after_first_layer(1, 1)
        scatters = [(b, r) for b in range(BLOCKS) for r in range(ROW_BLOCKS)]
        for (b, r), tag in zip(scatters, ("staged_first", "silu_a10", "silu_a11", "grouped10")):
            stage_rows(0, b, r, tag)

        for r in range(ROW_BLOCKS):
            for e in range(E):
                for b in range(BLOCKS):
                    first = e * C + b * P
                    nc.vector.tensor_tensor(
                        results[r][:].indirect(listed(first, P)), staged[e, b, r], gates[:, first : first + P], MULT
                    )
            nc.sync.dma_start(out=out[r * P : (r + 1) * P, :], in_=results[r][:])
